import numpy as np
import ml_dtypes


def mxq(x, axis, fmt="e4m3"):
    dtype, down = {"e4m3": (ml_dtypes.float8_e4m3fn, 7), "e5m2": (ml_dtypes.float8_e5m2, 14)}[fmt]
    v = np.moveaxis(np.asarray(x, np.float32).astype(ml_dtypes.bfloat16).astype(np.float64), axis, -1)
    blocks = v.reshape(v.shape[:-1] + (-1, 32))
    amax = np.abs(blocks).max(-1, keepdims=True)
    byte = np.maximum(np.where(amax > 0, np.frexp(amax)[1] - 1 + 127, 0) - down, 1)
    scale = np.exp2(byte - 127.0)
    codes = (blocks / scale).astype(np.float32).astype(dtype).astype(np.float64)
    return np.moveaxis((codes * scale).reshape(v.shape), -1, axis)


WIDE = False


def mx_kscale(k):
    if not WIDE:
        return np.ones(k)
    levels = np.array([10, -10, 5, -5, 0])
    if k % 512:
        return np.exp2(np.random.permutation(np.resize(levels, k // 32))).repeat(32)
    a = np.empty((k // 512, 16))
    for p in range(k // 512):
        a[p, :8] = np.random.permutation(np.resize(levels, 8))
        for g in range(8):
            far = levels[np.abs(levels - a[p, g]) >= 10]
            a[p, g + 8] = far[np.random.randint(len(far))]
    return np.exp2(a.ravel()).repeat(32)


def f64(x):
    return np.asarray(x).astype(np.float64)


def striped(idx):
    return np.tile(np.asarray(idx).reshape(-1, 16).T, (8, 1)).astype(np.uint16)


def unstriped(offs):
    return offs[:16].T.reshape(-1).astype(np.int64)


E2M1 = np.array([0.0, 0.5, 1.0, 1.5, 2.0, 3.0, 4.0, 6.0, -0.0, -0.5, -1.0, -1.5, -2.0, -3.0, -4.0, -6.0])


def pack_weight(w, fmt):
    k, n = w.shape
    w = f64(np.asarray(w, np.float32).astype(ml_dtypes.bfloat16)).reshape(k // 32, 32, n)
    amax = np.abs(w).max(1)
    if fmt == "e4m3":
        byte = np.frexp(amax)[1] - 1 + 127 - 7
    else:
        mant, ex = np.frexp(amax / 6.0)
        byte = np.where(mant > 0.5, ex, ex - 1) + 127
    byte = np.clip(np.where(amax > 0, byte, 1), 1, 254)
    scaled = (w * np.exp2(127.0 - byte)[:, None, :]).reshape(k, n).astype(np.float32)
    by_word = np.ascontiguousarray(scaled.reshape(k // 512, 128, 4, n).transpose(0, 1, 3, 2))
    if fmt == "e4m3":
        words = by_word.astype(ml_dtypes.float8_e4m3fn).view(np.uint8)
    else:
        c = by_word.astype(ml_dtypes.float4_e2m1fn).view(np.uint8) & 0xF
        words = (c[..., 0::2] | (c[..., 1::2] << 4)).reshape(k // 512, 128, 2 * n)
    return np.ascontiguousarray(words), np.ascontiguousarray(byte.astype(np.uint8).reshape(k // 512, 16, n))


def unpack_weight(words, scales, fmt):
    g, _, n = scales.shape
    words = np.ascontiguousarray(words).reshape(g, 128, n, -1)
    if fmt == "e4m3":
        vals = words.view(ml_dtypes.float8_e4m3fn).astype(np.float64)
    else:
        nib = np.empty((g, 128, n, 4), np.uint8)
        nib[..., 0::2] = words & 0xF
        nib[..., 1::2] = words >> 4
        vals = E2M1[nib]
    vals = vals * np.repeat(np.exp2(scales.astype(np.float64) - 127.0), 8, axis=1)[..., None]
    return vals.transpose(0, 1, 3, 2).reshape(g * 512, n)


def softplus(v):
    return np.log(1.0 + np.exp(v))


B, N, T, D, NQ = 1, 512, 2048, 1024, 128


def setup_inputs():
    n = np.random.standard_normal
    idx = np.random.permutation(T)[:B * N]
    s = mx_kscale(D)[:, None]
    kp = pack_weight(n((D, T)) / s, "e2m1")
    cp = pack_weight(n((D, T)) / s / 12, "e4m3")
    return {
        "qT": (n((B, D, NQ)) * s * (1.00 / np.sqrt(D))).astype(np.float32),
        "k_words": np.ascontiguousarray(kp[0].reshape(1, 2, 128, T, 2).transpose(0, 2, 3, 1, 4)).reshape(1, 128, T, 4),
        "k_scales": kp[1],
        "c_words": cp[0],
        "c_scales": cp[1],
        "ps": (n((B, NQ, 1)) + 1).astype(np.float32),
        "offs": striped(idx),
    }


def reference(qT, k_words, k_scales, c_words, c_scales, ps, offs):
    idx = unstriped(offs)
    pick = lambda x, which: x[:, which].reshape(x.shape[0], B, -1).transpose(1, 0, 2)
    k = unpack_weight(k_words.reshape(1, 128, T, 2, 2).transpose(0, 3, 1, 2, 4).reshape(2, 128, 2 * T), k_scales, "e2m1")
    kg = pick(k, idx)
    c = unpack_weight(c_words, c_scales, "e4m3")
    cg = pick(c, idx)
    qq = mxq(f64(qT), 1, "e4m3")
    a = (qq.transpose(0, 2, 1) @ kg) + (qq.transpose(0, 2, 1) @ cg)
    y = softplus(a - f64(ps))
    return y

@@ -1,0 +1,135 @@
+from contextlib import ExitStack
+
+import concourse.mybir as mybir
+
+N, T, D, NQ = 512, 2048, 1024, 128
+FLOPS = 2 * 2 * NQ * D * N
+
+F32 = mybir.dt.float32
+BF16 = mybir.dt.bfloat16
+I32 = mybir.dt.int32
+U32 = mybir.dt.uint32
+U16 = mybir.dt.uint16
+U8 = mybir.dt.uint8
+FP8X4 = mybir.dt.float8_e4m3fn_x4
+FP4X4 = mybir.dt.float4_e2m1fn_x4
+ACT = mybir.ActivationFunctionType
+ALU = mybir.AluOpType
+
+P = 128
+PACK = 4
+PASSES = 2
+QUAD = 32
+COLS = 128
+GROUPS = N // COLS
+HALF = N // 2
+EXP_CAP = 2.0 ** 60
+
+
+def tile_attend_residlse_topk_kernel(tc, qT, k_words, k_scales, c_words, c_scales, ps, offs, out):
+    nc = tc.nc
+    with ExitStack() as ctx:
+        sb = ctx.enter_context(tc.tile_pool(name="sb", bufs=1))
+        psum = ctx.enter_context(tc.psum_pool(name="psum", bufs=1))
+
+        q_raw = sb.tile([P, PASSES, PACK, NQ], F32, name="q_raw")
+        nc.sync.dma_start(q_raw[:], qT[0].rearrange("(g p j) w -> p g j w", g=PASSES, j=PACK))
+        offsets = sb.tile([P, N // 16], U16, name="offsets")
+        nc.sync.dma_start(offsets[:], offs)
+        ps_col = sb.tile([P, 1], F32, name="ps_col")
+        nc.sync.dma_start(ps_col[:], ps[0])
+
+        ks_win = sb.tile([P, T], U8, name="ks_win", align_bytes=64)
+        cs_win = sb.tile([P, T], U8, name="cs_win", align_bytes=64)
+        ks_odd = sb.tile([P, N], U8, name="ks_odd", align_bytes=64)
+        nc.vector.memset(ks_win[:].bitcast(I32), 0)
+        nc.vector.memset(cs_win[:].bitcast(I32), 0)
+        nc.vector.memset(ks_odd[:].bitcast(I32), 0)
+
+        ks_rows = k_scales.rearrange("o (q r) t -> r q o t", r=PACK)
+        for r in range(PACK):
+            nc.sync.dma_start(ks_win[r:P:16, :].bitcast(I32), ks_rows[r].bitcast(I32))
+        kw_win = sb.tile([P, T], I32, name="kw_win", align_bytes=64)
+        nc.sync.dma_start(kw_win[:], k_words[0].rearrange("p t b -> p (t b)").bitcast(I32))
+        for quad in range(P // QUAD):
+            nc.sync.dma_start(
+                cs_win[QUAD * quad + 4 : QUAD * quad + 12, :].bitcast(I32),
+                c_scales[:, 4 * quad : 4 * quad + 4, :].bitcast(I32),
+            )
+        cw_win = [sb.tile([P, T], I32, name="cw_win%d" % g, align_bytes=64) for g in range(PASSES)]
+        for g in range(PASSES):
+            nc.sync.dma_start(cw_win[g][:], c_words[g].rearrange("p t b -> p (t b)").bitcast(I32))
+        neg_ps = sb.tile([P, 1], F32, name="neg_ps")
+        nc.scalar.mul(neg_ps[:], ps_col[:], -1.0)
+        q_bf = sb.tile([P, PASSES, NQ, PACK], BF16, name="q_bf", align_bytes=64)
+        nc.scalar.copy(q_bf[:], q_raw[:].rearrange("p g j w -> p g w j"))
+
+        ks = sb.tile([P, N], U8, name="ks", align_bytes=64)
+        nc.vector.tensor_copy(ks[:], ks_win[:].indirect(offsets[:]))
+        nc.scalar.dma_start(ks_odd[0:112, :].bitcast(I32), ks[16:P, :].bitcast(I32))
+
+        q_codes = sb.tile([P, PASSES * NQ], U32, name="q_codes", align_bytes=64)
+        q_scales = sb.tile([P, PASSES * NQ], U8, name="q_scales", align_bytes=64)
+        nc.vector.quantize_mx(
+            out=q_codes[:].bitcast(FP8X4),
+            scales=q_scales[:],
+            in_=q_bf[:].rearrange("p g w j -> p (g w j)"),
+        )
+
+        kw_pairs = sb.tile([P, N], U32, name="kw_pairs", align_bytes=64)
+        nc.vector.tensor_copy(kw_pairs[:], kw_win[:].bitcast(U32).indirect(offsets[:]))
+        kw = sb.tile([P, PASSES, N], U16, name="kw", align_bytes=64)
+        nc.vector.tensor_copy(kw[:], kw_pairs[:].bitcast(U16).rearrange("p (n g) -> p g n", g=PASSES))
+
+        cs = sb.tile([P, N], U8, name="cs", align_bytes=64)
+        nc.vector.tensor_copy(cs[:], cs_win[:].indirect(offsets[:]))
+
+        cw0 = sb.tile([P, N], U32, name="cw0", align_bytes=64)
+        nc.vector.tensor_copy(cw0[:], cw_win[0][:].bitcast(U32).indirect(offsets[:]))
+        cw1 = [sb.tile([P, HALF], U32, name="cw1_%d" % h, align_bytes=64) for h in range(2)]
+        for h in range(2):
+            half_list = offsets[:, h * HALF // 16 : (h + 1) * HALF // 16]
+            nc.vector.tensor_copy(cw1[h][:], cw_win[1][:].bitcast(U32).indirect(half_list))
+
+        acc = [psum.tile([P, COLS], F32, name="acc%d" % j) for j in range(GROUPS)]
+
+        def score_pass(j, g, words, scales, start, stop):
+            nc.tensor.matmul_mx(
+                out=acc[j][:],
+                lhsT=q_codes[:, g * NQ : (g + 1) * NQ].bitcast(FP8X4),
+                lhsT_scale=q_scales[:, g * NQ : (g + 1) * NQ],
+                rhs=words,
+                rhs_scale=scales,
+                start=start,
+                stop=stop,
+            )
+
+        k_planes = [ks, ks_odd]
+        for g in range(PASSES):
+            for j in range(GROUPS):
+                cols = slice(j * COLS, (j + 1) * COLS)
+                score_pass(j, g, kw[:, g, cols].bitcast(FP4X4), k_planes[g][:, cols], g == 0, False)
+        for j in range(GROUPS):
+            cols = slice(j * COLS, (j + 1) * COLS)
+            score_pass(j, 0, cw0[:, cols].bitcast(FP8X4), cs[4:P, cols], False, False)
+        for j in range(GROUPS):
+            cols = slice(j * COLS, (j + 1) * COLS)
+            in_half = slice((j % 2) * COLS, (j % 2 + 1) * COLS)
+            score_pass(j, 1, cw1[j // 2][:, in_half].bitcast(FP8X4), cs[8:P, cols], False, True)
+
+        ex = sb.tile([P, N], F32, name="ex")
+        for j in range(GROUPS):
+            nc.scalar.activation(ex[:, j * COLS : (j + 1) * COLS], acc[j][:], ACT.Exp, bias=neg_ps[:])
+        one_plus = sb.tile([P, N], F32, name="one_plus")
+        for h in range(2):
+            half = slice(h * HALF, (h + 1) * HALF)
+            nc.vector.tensor_scalar(one_plus[:, half], ex[:, half], EXP_CAP, 1.0, ALU.min, ALU.add)
+        lg = sb.tile([P, N], F32, name="lg")
+        res = sb.tile([P, N], F32, name="res")
+        for j in range(GROUPS):
+            cols = slice(j * COLS, (j + 1) * COLS)
+            nc.scalar.activation(lg[:, cols], one_plus[:, cols], ACT.Ln)
+            nc.vector.scalar_tensor_tensor(res[:, cols], acc[j][:], neg_ps[:], lg[:, cols], ALU.add, ALU.max)
+        for h in range(2):
+            half = slice(h * HALF, (h + 1) * HALF)
+            nc.sync.dma_start(out[0][:, half], res[:, half])

@@ -40,7 +40,7 @@ def tile_attend_residlse_topk_kernel(tc, qT, k_words, k_scales, c_words, c_scale
         nc.sync.dma_start(ps_col[:], ps[0])
 
         ks_win = sb.tile([P, T], U8, name="ks_win", align_bytes=64)
-        cs_win = sb.tile([P, T], U8, name="cs_win", align_bytes=64)
+        cs_win = sb.tile([P, T], U8, name="cs_win", tag="scales_then_pairs", align_bytes=64)
         ks_odd = sb.tile([P, N], U8, name="ks_odd", align_bytes=64)
         nc.vector.memset(ks_win[:].bitcast(I32), 0)
         nc.vector.memset(cs_win[:].bitcast(I32), 0)
@@ -51,11 +51,7 @@ def tile_attend_residlse_topk_kernel(tc, qT, k_words, k_scales, c_words, c_scale
             nc.sync.dma_start(ks_win[r:P:16, :].bitcast(I32), ks_rows[r].bitcast(I32))
         kw_win = sb.tile([P, T], I32, name="kw_win", align_bytes=64)
         nc.sync.dma_start(kw_win[:], k_words[0].rearrange("p t b -> p (t b)").bitcast(I32))
-        for quad in range(P // QUAD):
-            nc.sync.dma_start(
-                cs_win[QUAD * quad + 4 : QUAD * quad + 12, :].bitcast(I32),
-                c_scales[:, 4 * quad : 4 * quad + 4, :].bitcast(I32),
-            )
+        nc.sync.dma_start(cs_win[32:96:2, :].bitcast(I32), c_scales.rearrange("o f t -> f o t").bitcast(I32))
         cw_win = [sb.tile([P, T], I32, name="cw_win%d" % g, align_bytes=64) for g in range(PASSES)]
         for g in range(PASSES):
             nc.sync.dma_start(cw_win[g][:], c_words[g].rearrange("p t b -> p (t b)").bitcast(I32))
@@ -76,15 +72,18 @@ def tile_attend_residlse_topk_kernel(tc, qT, k_words, k_scales, c_words, c_scale
             in_=q_bf[:].rearrange("p g w j -> p (g w j)"),
         )
 
-        kw_pairs = sb.tile([P, N], U32, name="kw_pairs", align_bytes=64)
+        cs_rows = sb.tile([P, N], U8, name="cs_rows", align_bytes=64)
+        nc.vector.tensor_copy(cs_rows[:], cs_win[:].indirect(offsets[:]))
+        cs = sb.tile([P, N], U8, name="cs", align_bytes=64)
+        for r in range(PACK):
+            nc.scalar.dma_start(cs[r:P:4, :].bitcast(I32), cs_rows[32 + 4 * r : 96 + 4 * r : 2, :].bitcast(I32))
+
+        kw_pairs = sb.tile([P, N], U32, name="kw_pairs", tag="scales_then_pairs", align_bytes=64)
         nc.vector.tensor_copy(kw_pairs[:], kw_win[:].bitcast(U32).indirect(offsets[:]))
         kw = sb.tile([P, PASSES, N], U16, name="kw", align_bytes=64)
         nc.vector.tensor_copy(kw[:], kw_pairs[:].bitcast(U16).rearrange("p (n g) -> p g n", g=PASSES))
 
-        cs = sb.tile([P, N], U8, name="cs", align_bytes=64)
-        nc.vector.tensor_copy(cs[:], cs_win[:].indirect(offsets[:]))
-
-        cw0 = sb.tile([P, N], U32, name="cw0", align_bytes=64)
+        cw0 = sb.tile([P, N], U32, name="cw0", tag="scales_then_pairs", align_bytes=64)
         nc.vector.tensor_copy(cw0[:], cw_win[0][:].bitcast(U32).indirect(offsets[:]))
         cw1 = [sb.tile([P, HALF], U32, name="cw1_%d" % h, align_bytes=64) for h in range(2)]
         for h in range(2):
@@ -111,11 +110,11 @@ def tile_attend_residlse_topk_kernel(tc, qT, k_words, k_scales, c_words, c_scale
                 score_pass(j, g, kw[:, g, cols].bitcast(FP4X4), k_planes[g][:, cols], g == 0, False)
         for j in range(GROUPS):
             cols = slice(j * COLS, (j + 1) * COLS)
-            score_pass(j, 0, cw0[:, cols].bitcast(FP8X4), cs[4:P, cols], False, False)
+            score_pass(j, 0, cw0[:, cols].bitcast(FP8X4), cs[:, cols], False, False)
         for j in range(GROUPS):
             cols = slice(j * COLS, (j + 1) * COLS)
             in_half = slice((j % 2) * COLS, (j % 2 + 1) * COLS)
-            score_pass(j, 1, cw1[j // 2][:, in_half].bitcast(FP8X4), cs[8:P, cols], False, True)
+            score_pass(j, 1, cw1[j // 2][:, in_half].bitcast(FP8X4), cs[4:P, cols], False, True)
 
         ex = sb.tile([P, N], F32, name="ex")
         for j in range(GROUPS):

from contextlib import ExitStack

import concourse.mybir as mybir

N, T, D, NQ = 512, 2048, 1024, 128
FLOPS = 2 * 2 * NQ * D * N

F32 = mybir.dt.float32
BF16 = mybir.dt.bfloat16
I32 = mybir.dt.int32
U32 = mybir.dt.uint32
U16 = mybir.dt.uint16
U8 = mybir.dt.uint8
FP8X4 = mybir.dt.float8_e4m3fn_x4
FP4X4 = mybir.dt.float4_e2m1fn_x4
ACT = mybir.ActivationFunctionType
ALU = mybir.AluOpType

P = 128
PACK = 4
PASSES = 2
QUAD = 32
COLS = 128
GROUPS = N // COLS
HALF = N // 2
EXP_CAP = 2.0 ** 60


def tile_attend_residlse_topk_kernel(tc, qT, k_words, k_scales, c_words, c_scales, ps, offs, out):
    nc = tc.nc
    with ExitStack() as ctx:
        sb = ctx.enter_context(tc.tile_pool(name="sb", bufs=1))
        psum = ctx.enter_context(tc.psum_pool(name="psum", bufs=1))

        q_raw = sb.tile([P, PASSES, PACK, NQ], F32, name="q_raw")
        nc.sync.dma_start(q_raw[:], qT[0].rearrange("(g p j) w -> p g j w", g=PASSES, j=PACK))
        offsets = sb.tile([P, N // 16], U16, name="offsets")
        nc.sync.dma_start(offsets[:], offs)
        ps_col = sb.tile([P, 1], F32, name="ps_col")
        nc.sync.dma_start(ps_col[:], ps[0])

        ks_win = sb.tile([P, T], U8, name="ks_win", align_bytes=64)
        cs_win = sb.tile([P, T], U8, name="cs_win", tag="scales_then_pairs", align_bytes=64)
        ks_odd = sb.tile([P, N], U8, name="ks_odd", align_bytes=64)
        nc.vector.memset(ks_win[:].bitcast(I32), 0)
        nc.vector.memset(cs_win[:].bitcast(I32), 0)
        nc.vector.memset(ks_odd[:].bitcast(I32), 0)

        ks_rows = k_scales.rearrange("o (q r) t -> r q o t", r=PACK)
        for r in range(PACK):
            nc.sync.dma_start(ks_win[r:P:16, :].bitcast(I32), ks_rows[r].bitcast(I32))
        kw_win = sb.tile([P, T], I32, name="kw_win", align_bytes=64)
        nc.sync.dma_start(kw_win[:], k_words[0].rearrange("p t b -> p (t b)").bitcast(I32))
        nc.sync.dma_start(cs_win[32:96:2, :].bitcast(I32), c_scales.rearrange("o f t -> f o t").bitcast(I32))
        cw_win = [sb.tile([P, T], I32, name="cw_win%d" % g, align_bytes=64) for g in range(PASSES)]
        for g in range(PASSES):
            nc.sync.dma_start(cw_win[g][:], c_words[g].rearrange("p t b -> p (t b)").bitcast(I32))
        neg_ps = sb.tile([P, 1], F32, name="neg_ps")
        nc.scalar.mul(neg_ps[:], ps_col[:], -1.0)
        q_bf = sb.tile([P, PASSES, NQ, PACK], BF16, name="q_bf", align_bytes=64)
        nc.scalar.copy(q_bf[:], q_raw[:].rearrange("p g j w -> p g w j"))

        ks = sb.tile([P, N], U8, name="ks", align_bytes=64)
        nc.vector.tensor_copy(ks[:], ks_win[:].indirect(offsets[:]))
        nc.scalar.dma_start(ks_odd[0:112, :].bitcast(I32), ks[16:P, :].bitcast(I32))

        q_codes = sb.tile([P, PASSES * NQ], U32, name="q_codes", align_bytes=64)
        q_scales = sb.tile([P, PASSES * NQ], U8, name="q_scales", align_bytes=64)
        nc.vector.quantize_mx(
            out=q_codes[:].bitcast(FP8X4),
            scales=q_scales[:],
            in_=q_bf[:].rearrange("p g w j -> p (g w j)"),
        )

        cs_rows = sb.tile([P, N], U8, name="cs_rows", align_bytes=64)
        nc.vector.tensor_copy(cs_rows[:], cs_win[:].indirect(offsets[:]))
        cs = sb.tile([P, N], U8, name="cs", align_bytes=64)
        for r in range(PACK):
            nc.scalar.dma_start(cs[r:P:4, :].bitcast(I32), cs_rows[32 + 4 * r : 96 + 4 * r : 2, :].bitcast(I32))

        kw_pairs = sb.tile([P, N], U32, name="kw_pairs", tag="scales_then_pairs", align_bytes=64)
        nc.vector.tensor_copy(kw_pairs[:], kw_win[:].bitcast(U32).indirect(offsets[:]))
        kw = sb.tile([P, PASSES, N], U16, name="kw", align_bytes=64)
        nc.vector.tensor_copy(kw[:], kw_pairs[:].bitcast(U16).rearrange("p (n g) -> p g n", g=PASSES))

        cw0 = sb.tile([P, N], U32, name="cw0", tag="scales_then_pairs", align_bytes=64)
        nc.vector.tensor_copy(cw0[:], cw_win[0][:].bitcast(U32).indirect(offsets[:]))
        cw1 = [sb.tile([P, HALF], U32, name="cw1_%d" % h, align_bytes=64) for h in range(2)]
        for h in range(2):
            half_list = offsets[:, h * HALF // 16 : (h + 1) * HALF // 16]
            nc.vector.tensor_copy(cw1[h][:], cw_win[1][:].bitcast(U32).indirect(half_list))

        acc = [psum.tile([P, COLS], F32, name="acc%d" % j) for j in range(GROUPS)]

        def score_pass(j, g, words, scales, start, stop):
            nc.tensor.matmul_mx(
                out=acc[j][:],
                lhsT=q_codes[:, g * NQ : (g + 1) * NQ].bitcast(FP8X4),
                lhsT_scale=q_scales[:, g * NQ : (g + 1) * NQ],
                rhs=words,
                rhs_scale=scales,
                start=start,
                stop=stop,
            )

        k_planes = [ks, ks_odd]
        for g in range(PASSES):
            for j in range(GROUPS):
                cols = slice(j * COLS, (j + 1) * COLS)
                score_pass(j, g, kw[:, g, cols].bitcast(FP4X4), k_planes[g][:, cols], g == 0, False)
        for j in range(GROUPS):
            cols = slice(j * COLS, (j + 1) * COLS)
            score_pass(j, 0, cw0[:, cols].bitcast(FP8X4), cs[:, cols], False, False)
        for j in range(GROUPS):
            cols = slice(j * COLS, (j + 1) * COLS)
            in_half = slice((j % 2) * COLS, (j % 2 + 1) * COLS)
            score_pass(j, 1, cw1[j // 2][:, in_half].bitcast(FP8X4), cs[4:P, cols], False, True)

        ex = sb.tile([P, N], F32, name="ex")
        for j in range(GROUPS):
            nc.scalar.activation(ex[:, j * COLS : (j + 1) * COLS], acc[j][:], ACT.Exp, bias=neg_ps[:])
        one_plus = sb.tile([P, N], F32, name="one_plus")
        for h in range(2):
            half = slice(h * HALF, (h + 1) * HALF)
            nc.vector.tensor_scalar(one_plus[:, half], ex[:, half], EXP_CAP, 1.0, ALU.min, ALU.add)
        lg = sb.tile([P, N], F32, name="lg")
        res = sb.tile([P, N], F32, name="res")
        for j in range(GROUPS):
            cols = slice(j * COLS, (j + 1) * COLS)
            nc.scalar.activation(lg[:, cols], one_plus[:, cols], ACT.Ln)
            nc.vector.scalar_tensor_tensor(res[:, cols], acc[j][:], neg_ps[:], lg[:, cols], ALU.add, ALU.max)
        for h in range(2):
            half = slice(h * HALF, (h + 1) * HALF)
            nc.sync.dma_start(out[0][:, half], res[:, half])
